import numpy as np, ml_dtypes
CORES = [19,147,275,403]
N = 4
NP, TK = 2, 128
def setup_inputs(rng):
    return {"x": rng.standard_normal((N, 128, TK), dtype=np.float32).astype(ml_dtypes.bfloat16), "w1": (rng.standard_normal((N, 128, 128), dtype=np.float32) / 8).astype(ml_dtypes.bfloat16), "w2": (rng.standard_normal((N, 128, NP * 128), dtype=np.float32) / 8).astype(ml_dtypes.bfloat16)}
def setup_inputs_big(rng):
    d = setup_inputs(rng)
    for k in ("x", "w1", "w2"): d[k] = (d[k].astype(np.float32) * 1024.0).astype(d[k].dtype)
    return d
def setup_inputs_small(rng):
    d = setup_inputs(rng)
    for k in ("x", "w1", "w2"): d[k] = (d[k].astype(np.float32) * (1 / 1024.0)).astype(d[k].dtype)
    return d
def setup_inputs_apart(rng):
    d = setup_inputs(rng)
    f = (10.0 ** rng.permutation(np.linspace(-1.5, 1.5, N))).astype(np.float32).reshape(N, 1, 1)
    for k in ("x", "w1", "w2"): d[k] = (d[k].astype(np.float32) * f).astype(d[k].dtype)
    return d
def reference(x, w1, w2):
    X, W1, W2 = x.astype(np.float64), w1.astype(np.float64), w2.astype(np.float64)
    h = [np.maximum(W1[p].T @ X[p], 0.0) for p in range(NP)]
    y = np.full((N, 128, TK), np.nan)
    for q in range(NP, N):
        y[q] = sum(W2[q][:, 128 * p:128 * p + 128].T @ h[p] for p in range(NP))
    return {"y": y.astype(ml_dtypes.bfloat16 if x.dtype != np.float64 else np.float64)}

from concourse.mybir import AluOpType

TK = 128
SCRATCH = {
    "xs": ("sbuf", [128, TK], "bfloat16"),
    "w1s": ("sbuf", [128, 128], "bfloat16"),
    "w2s": ("sbuf", [128, 256], "bfloat16"),
    "zero": ("sbuf", [128, TK], "bfloat16"),
    "ha": ("sbuf", [128, TK], "bfloat16"),
    "hb": ("sbuf", [128, TK], "bfloat16"),
    "ys": ("sbuf", [128, TK], "bfloat16"),
    "ps": ("psum", [128, TK], "float32"),
}
SEMAPHORES = ["ld", "zs", "mm", "act", "peer", "direct", "relay", "sent", "cp", "st"]


def _engines(mask):
    return bin(mask).count("1")


def _routes(T, topo):
    cores = T.cores
    n_p = T.w2.shape[1] // 128
    out = []
    for q in range(n_p, len(cores)):
        for p in range(n_p):
            if topo.may_write(cores[p], cores[q]):
                out.append((p, None, q))
            else:
                r = [r for r in range(n_p) if r != p and topo.may_write(cores[p], cores[r])
                     and topo.may_write(cores[r], cores[q])][0]
                out.append((p, r, q))
    return n_p, out


def rank_program(g, core, T, topo):
    me = T.rank_of(core)
    if me is None:
        return
    S = T.sem
    cores = T.cores
    n_p, routes = _routes(T, topo)

    def send(dst_rank, out, in_, sem):
        d = cores[dst_rank]
        rid, pid = topo.addr(d, core)
        m = topo.mask(core, d)
        g.remote_dma(out, in_, remote_sem=sem, local_sem=S.sent, pid=pid, routing_id=rid, dma_engine_mask=m)
        return _engines(m)

    if me < n_p:
        g.sync.dma_start(T.xs[:], T.x[:]).then_inc(S.ld, 16)
        g.scalar.dma_start(T.w1s[:], T.w1[:]).then_inc(S.ld, 16)
        g.vector.memset(T.zero[:], 0.0).then_inc(S.zs, 1)
        g.tensor.wait_ge(S.ld, 32)
        g.tensor.matmul(T.ps[:], T.w1s[:], T.xs[:], True, True).then_inc(S.mm, 1)
        g.vector.wait_ge(S.zs, 1)
        g.vector.wait_ge(S.mm, 1)
        g.vector.tensor_tensor(T.ha[:], T.ps[:], T.zero[:], AluOpType.max).then_inc(S.act, 1)

        g.wait_ge(S.act, 1)
        left = 0
        for (p, r, q) in routes:
            if p == me and r is not None:
                left += send(r, T.hb[:], T.ha[:], S.peer)
        for (p, r, q) in routes:
            if p == me and r is None:
                left += send(q, T.ha[:], T.ha[:], S.direct)
        for (p, r, q) in routes:
            if r == me:
                g.wait_ge(S.peer, _engines(topo.mask(cores[p], core)))
                left += send(q, T.hb[:], T.hb[:], S.relay)
        g.wait_ge(S.sent, left)
    else:
        g.sync.dma_start(T.w2s[:], T.w2[:]).then_inc(S.ld, 16)
        (pa, _, _), = [t for t in routes if t[2] == me and t[1] is None]
        (pb, rb, _), = [t for t in routes if t[2] == me and t[1] is not None]
        g.tensor.wait_ge(S.ld, 16)
        g.tensor.wait_ge(S.direct, _engines(topo.mask(cores[pa], core)))
        g.tensor.matmul(T.ps[:], T.w2s[:, 128 * pa:128 * pa + 128], T.ha[:], True, False)
        g.tensor.wait_ge(S.relay, _engines(topo.mask(cores[rb], core)))
        g.tensor.matmul(T.ps[:], T.w2s[:, 128 * pb:128 * pb + 128], T.hb[:], False, True).then_inc(S.mm, 1)
        g.vector.wait_ge(S.mm, 1)
        g.vector.tensor_copy(T.ys[:], T.ps[:]).then_inc(S.cp, 1)
        g.sync.wait_ge(S.cp, 1)
        g.sync.dma_start(T.y[:], T.ys[:]).then_inc(S.st, 16)
        g.sync.wait_ge(S.st, 16)
